import numpy as np, ml_dtypes
CORES = [76,84,92,100,108,116,124]
N = 7
W, KW = 512, 5
H = KW // 2
def setup_inputs(rng):
    return {"x": rng.standard_normal((N, 128, W), dtype=np.float32).astype(ml_dtypes.bfloat16), "t": rng.standard_normal((N, 128, KW * W), dtype=np.float32).astype(ml_dtypes.bfloat16)}
def setup_inputs_big(rng):
    d = setup_inputs(rng)
    for k in ("x", "t"): d[k] = (d[k].astype(np.float32) * 1024.0).astype(d[k].dtype)
    return d
def setup_inputs_small(rng):
    d = setup_inputs(rng)
    for k in ("x", "t"): d[k] = (d[k].astype(np.float32) * (1 / 1024.0)).astype(d[k].dtype)
    return d
def reference(x, t):
    X, T = x.astype(np.float64), t.astype(np.float64)
    g = np.concatenate(list(X), axis=1)
    p = np.concatenate([g[:, -H:], g, g[:, :H]], axis=1)
    y = np.stack([sum(T[r][:, W * i:W * i + W] * p[:, W * r + i:W * r + i + W] for i in range(KW)) for r in range(N)])
    return {"y": y.astype(ml_dtypes.bfloat16 if x.dtype != np.float64 else np.float64)}

@@ -1,0 +1,150 @@
+from concourse.bass import DstId, RemoteDMATransfer
+from concourse.mybir import AluOpType
+
+W, KW = 512, 5
+H = KW // 2
+PRELOAD = 2
+
+SCRATCH = {
+    "ed": ("dram", [2, 128, H], "bfloat16"),
+    "rl": ("dram", [128, H], "bfloat16"),
+    "hd": ("dram", [2, 128, H], "bfloat16"),
+    "hb": ("sbuf", [128, 8], "bfloat16"),
+    "xs": ("sbuf", [128, W], "bfloat16"),
+    "ts": ("sbuf", [128, KW * W], "bfloat16"),
+    "pr": ("sbuf", [128, KW * W], "bfloat16"),
+    "ys": ("sbuf", [128, W], "bfloat16"),
+    "pa": ("sbuf", [128, 4], "float32"),
+    "pb": ("sbuf", [128, 4], "float32"),
+    "xp": ("psum", [128, 2 * W], "float32"),
+    "acc": ("psum", [128, W], "float32"),
+}
+SEMAPHORES = ["ed", "x", "t0", "t1", "t2", "t3", "t4", "sent", "rl", "hl", "hr", "hb", "v", "vd", "st"]
+
+
+def _engines(mask, n, skip=0):
+    bits = [b for b in range(mask.bit_length()) if (mask >> b) & 1]
+    m = 0
+    for b in bits[skip:skip + n]:
+        m |= 1 << b
+    return m
+
+
+def _routes(T, topo):
+    cores = list(T.cores)
+    n = len(cores)
+    used = set(cores)
+    out = []
+    for r, src in enumerate(cores):
+        for side in (0, 1):
+            dst = cores[(r + (1 if side else -1)) % n]
+            via = None
+            if not topo.may_write(src, dst):
+                cand = [h for h in range(topo.CHIPS * topo.CORES_PER_CHIP)
+                        if topo.chip(h) == topo.chip(src) and h not in used and topo.may_write(h, dst)]
+                cand.sort(key=lambda h: (topo.die(h) != topo.die(src), h))
+                via = cand[0]
+                used.add(via)
+            out.append((src, side, via, dst))
+    return out
+
+
+def _landing(T, side):
+    return (T.hd[1], T.sem.hr) if side == 0 else (T.hd[0], T.sem.hl)
+
+
+def rank_program(g, core, T, topo):
+    routes = _routes(T, topo)
+    sem = T.sem
+
+    for src, side, via, dst in routes:
+        if via == core:
+            rid, pid, _se = topo.addr(dst)
+            out_ap, rsem = _landing(T, side)
+            g.wait_ge(sem.rl, 1)
+            g.remote_dma(out_ap=out_ap, in_ap=T.rl[:], remote_sem=rsem, local_sem=sem.sent, pid=pid,
+                         routing_id=rid, dma_engine_mask=_engines(topo.mask(core, dst), 1))
+            g.wait_ge(sem.sent, 1)
+            return
+    if T.rank_of(core) is None:
+        return
+
+    S, A, V = g.sync, g.scalar, g.vector
+    tab = lambda b, i: b[:, W * i:W * i + W]
+
+    S.dma_start(T.ed[0], T.x[:, 0:H]).then_inc(sem.ed, 16)
+    A.dma_start(T.ed[1], T.x[:, W - H:W]).then_inc(sem.ed, 16)
+    S.dma_start(T.xs[:], T.x[:]).then_inc(sem.x, 16)
+    queues = [A, S]
+    for i in range(PRELOAD):
+        queues[i % 2].dma_start(tab(T.ts, i), tab(T.t, i)).then_inc(sem["t%d" % i], 16)
+
+    transfers = []
+    for src, side, via, dst in routes:
+        if src != core:
+            continue
+        first = dst if via is None else via
+        rid, pid, _se = topo.addr(first)
+        out_ap, rsem = _landing(T, side) if via is None else (T.rl[:], sem.rl)
+        transfers.append(RemoteDMATransfer(dst_ids=[DstId(rid=rid, pnc=pid)],
+                                           dma_engine_mask=_engines(topo.mask(core, first), 1, skip=side),
+                                           remote_sem=rsem, src=T.ed[side], dst=out_ap))
+    g.wait_ge(sem.ed, 32)
+    g.remote_dma_fused(transfers, local_sem=sem.sent)
+    g.wait_ge(sem.sent, len(transfers))
+
+    S.wait_ge(sem.sent, len(transfers))
+    A.wait_ge(sem.sent, len(transfers))
+    for i in range(PRELOAD, KW):
+        queues[(i + 1) % 2].dma_start(tab(T.ts, i), tab(T.t, i)).then_inc(sem["t%d" % i], 16)
+
+    S.wait_ge(sem.hl, 1)
+    S.dma_start(T.hb[:, 0:H], T.hd[0]).then_inc(sem.hb, 16)
+    A.wait_ge(sem.hr, 1)
+    A.dma_start(T.hb[:, H:2 * H], T.hd[1]).then_inc(sem.hb, 16)
+
+    issued = [0]
+
+    def done(ins):
+        ins.then_inc(sem.v, 1)
+        issued[0] += 1
+
+    def barrier():
+        V.wait_ge(sem.v, issued[0])
+
+    def tt(out, in0, in1, op):
+        return V.tensor_tensor(out=out, in0=in0, in1=in1, op=op)
+
+    mult, add = AluOpType.mult, AluOpType.add
+    done(V.memset(T.xp[:, 0:H], 0.0))
+    done(V.memset(T.xp[:, W + H:W + 2 * H], 0.0))
+    V.wait_ge(sem.x, 16)
+    done(V.tensor_copy(out=T.xp[:, H:W + H], in_=T.xs[:]))
+    barrier()
+    V.wait_ge(sem.t0, 16)
+    done(tt(T.acc[:], tab(T.ts, 0), T.xp[:, 0:W], mult))
+    V.wait_ge(sem.t1, 16)
+    done(tt(tab(T.pr, 1), tab(T.ts, 1), T.xp[:, 1:1 + W], mult))
+    for k in range(1, KW):
+        barrier()
+        if k < KW - 1:
+            done(tt(T.acc[:], T.acc[:], tab(T.pr, k), add))
+            V.wait_ge(sem["t%d" % (k + 1)], 16)
+            done(tt(tab(T.pr, k + 1), tab(T.ts, k + 1), T.xp[:, k + 1:k + 1 + W], mult))
+        else:
+            done(tt(T.ys[:], T.acc[:], tab(T.pr, k), add))
+
+    V.wait_ge(sem.hb, 32)
+    done(tt(T.pa[:, 0:2], T.ts[:, 0:2], T.hb[:, 0:2], mult))
+    done(tt(T.pa[:, 2:4], T.ts[:, KW * W - 2:KW * W], T.hb[:, 2:4], mult))
+    c1, c3 = W, 3 * W + W - 1
+    done(tt(T.pb[:, 0:2], T.ts[:, c1:c3 + 1:c3 - c1], T.hb[:, 1:3], mult))
+    barrier()
+    done(tt(T.pa[:, 0:4:3], T.pa[:, 0:4:3], T.pb[:, 0:2], add))
+    barrier()
+    tt(T.ys[:, 0:2], T.ys[:, 0:2], T.pa[:, 0:2], add).then_inc(sem.vd, 1)
+    tt(T.ys[:, W - 2:W], T.ys[:, W - 2:W], T.pa[:, 2:4], add).then_inc(sem.vd, 1)
+
+    S.wait_ge(sem.vd, 2)
+    S.dma_start(T.y[:], T.ys[:]).then_inc(sem.st, 16)
+    S.wait_ge(sem.st, 16)

@@ -3,12 +3,13 @@ from concourse.mybir import AluOpType
 
 W, KW = 512, 5
 H = KW // 2
-PRELOAD = 2
+NH = 4
+SLOT = {4: 0, 0: 1, 2: 2, 3: 3, 1: 4}
 
 SCRATCH = {
     "ed": ("dram", [2, 128, H], "bfloat16"),
     "rl": ("dram", [128, H], "bfloat16"),
-    "hd": ("dram", [2, 128, H], "bfloat16"),
+    "idd": ("dram", [1, 128 * 129], "bfloat16"),
     "hb": ("sbuf", [128, 8], "bfloat16"),
     "xs": ("sbuf", [128, W], "bfloat16"),
     "ts": ("sbuf", [128, KW * W], "bfloat16"),
@@ -16,10 +17,13 @@ SCRATCH = {
     "ys": ("sbuf", [128, W], "bfloat16"),
     "pa": ("sbuf", [128, 4], "float32"),
     "pb": ("sbuf", [128, 4], "float32"),
+    "zz": ("sbuf", [128, 136], "bfloat16"),
+    "idm": ("sbuf", [128, 128], "bfloat16"),
     "xp": ("psum", [128, 2 * W], "float32"),
     "acc": ("psum", [128, W], "float32"),
 }
-SEMAPHORES = ["ed", "x", "t0", "t1", "t2", "t3", "t4", "sent", "rl", "hl", "hr", "hb", "v", "vd", "st"]
+SEMAPHORES = ["ed", "x", "t0", "t1", "t2", "t3", "t4", "sent", "rl", "hb", "v", "vi", "vd", "st",
+              "ms", "i1", "idr", "p0", "p1", "p2", "p3", "pe"]
 
 
 def _engines(mask, n, skip=0):
@@ -50,7 +54,7 @@ def _routes(T, topo):
 
 
 def _landing(T, side):
-    return (T.hd[1], T.sem.hr) if side == 0 else (T.hd[0], T.sem.hl)
+    return T.hb[:, 0:H] if side == 0 else T.hb[:, H:2 * H]
 
 
 def rank_program(g, core, T, topo):
@@ -60,48 +64,57 @@ def rank_program(g, core, T, topo):
     for src, side, via, dst in routes:
         if via == core:
             rid, pid, _se = topo.addr(dst)
-            out_ap, rsem = _landing(T, side)
             g.wait_ge(sem.rl, 1)
-            g.remote_dma(out_ap=out_ap, in_ap=T.rl[:], remote_sem=rsem, local_sem=sem.sent, pid=pid,
-                         routing_id=rid, dma_engine_mask=_engines(topo.mask(core, dst), 1))
-            g.wait_ge(sem.sent, 1)
+            g.remote_dma(out_ap=_landing(T, side), in_ap=T.rl[:], remote_sem=sem.hb, local_sem=sem.sent, pid=pid,
+                         routing_id=rid, dma_engine_mask=_engines(topo.mask(core, dst), NH))
+            g.wait_ge(sem.sent, NH)
             return
     if T.rank_of(core) is None:
         return
 
-    S, A, V = g.sync, g.scalar, g.vector
-    tab = lambda b, i: b[:, W * i:W * i + W]
+    S, A, V, P = g.sync, g.scalar, g.vector, g.tensor
+    col = lambda b, j: b[:, W * j:W * j + W]
+
+    def load(q, i):
+        q.dma_start(col(T.ts, SLOT[i]), col(T.t, i)).then_inc(sem["t%d" % i], 16)
 
     S.dma_start(T.ed[0], T.x[:, 0:H]).then_inc(sem.ed, 16)
     A.dma_start(T.ed[1], T.x[:, W - H:W]).then_inc(sem.ed, 16)
     S.dma_start(T.xs[:], T.x[:]).then_inc(sem.x, 16)
-    queues = [A, S]
-    for i in range(PRELOAD):
-        queues[i % 2].dma_start(tab(T.ts, i), tab(T.t, i)).then_inc(sem["t%d" % i], 16)
+    A.wait_ge(sem.ms, 2)
+    A.dma_start(T.idd[0], T.zz[:, 0:129]).then_inc(sem.i1, 16)
+    load(A, 0)
+    load(A, 1)
+    load(A, 2)
+    A.wait_ge(sem.i1, 16)
+    A.dma_start(T.idm[:], T.idd[0, 0:128 * 128]).then_inc(sem.idr, 16)
+    load(A, 3)
+    load(A, 4)
 
+    mine = [r for r in routes if r[0] == core]
     transfers = []
-    for src, side, via, dst in routes:
-        if src != core:
-            continue
-        first = dst if via is None else via
-        rid, pid, _se = topo.addr(first)
-        out_ap, rsem = _landing(T, side) if via is None else (T.rl[:], sem.rl)
-        transfers.append(RemoteDMATransfer(dst_ids=[DstId(rid=rid, pnc=pid)],
-                                           dma_engine_mask=_engines(topo.mask(core, first), 1, skip=side),
-                                           remote_sem=rsem, src=T.ed[side], dst=out_ap))
+    for src, side, via, dst in mine:
+        if via is not None:
+            rid, pid, _se = topo.addr(via)
+            transfers.append(RemoteDMATransfer(dst_ids=[DstId(rid=rid, pnc=pid)],
+                                               dma_engine_mask=_engines(topo.mask(core, via), 1, skip=side),
+                                               remote_sem=sem.rl, src=T.ed[side], dst=T.rl[:]))
     g.wait_ge(sem.ed, 32)
     g.remote_dma_fused(transfers, local_sem=sem.sent)
-    g.wait_ge(sem.sent, len(transfers))
+    left = len(transfers)
+    for src, side, via, dst in mine:
+        if via is None:
+            rid, pid, _se = topo.addr(dst)
+            g.remote_dma(out_ap=_landing(T, side), in_ap=T.ed[side], remote_sem=sem.hb, local_sem=sem.sent, pid=pid,
+                         routing_id=rid, dma_engine_mask=_engines(topo.mask(core, dst), NH))
+            left += NH
+    g.wait_ge(sem.sent, left)
 
-    S.wait_ge(sem.sent, len(transfers))
-    A.wait_ge(sem.sent, len(transfers))
-    for i in range(PRELOAD, KW):
-        queues[(i + 1) % 2].dma_start(tab(T.ts, i), tab(T.t, i)).then_inc(sem["t%d" % i], 16)
-
-    S.wait_ge(sem.hl, 1)
-    S.dma_start(T.hb[:, 0:H], T.hd[0]).then_inc(sem.hb, 16)
-    A.wait_ge(sem.hr, 1)
-    A.dma_start(T.hb[:, H:2 * H], T.hd[1]).then_inc(sem.hb, 16)
+    P.wait_ge(sem.idr, 16)
+    for j in range(KW - 1):
+        P.wait_ge(sem["p%d" % j], 1)
+        mm = P.matmul(out=T.acc[:], lhsT=T.idm[:], rhs=col(T.pr, j), start=(j == 0), stop=(j == KW - 2))
+    mm.then_inc(sem.pe, 1)
 
     issued = [0]
 
@@ -116,35 +129,38 @@ def rank_program(g, core, T, topo):
         return V.tensor_tensor(out=out, in0=in0, in1=in1, op=op)
 
     mult, add = AluOpType.mult, AluOpType.add
+    V.memset(T.zz[:, 1:129], 0.0).then_inc(sem.ms, 1)
+    V.memset(T.zz[:, 0:1], 1.0).then_inc(sem.ms, 1)
     done(V.memset(T.xp[:, 0:H], 0.0))
     done(V.memset(T.xp[:, W + H:W + 2 * H], 0.0))
     V.wait_ge(sem.x, 16)
     done(V.tensor_copy(out=T.xp[:, H:W + H], in_=T.xs[:]))
     barrier()
-    V.wait_ge(sem.t0, 16)
-    done(tt(T.acc[:], tab(T.ts, 0), T.xp[:, 0:W], mult))
-    V.wait_ge(sem.t1, 16)
-    done(tt(tab(T.pr, 1), tab(T.ts, 1), T.xp[:, 1:1 + W], mult))
-    for k in range(1, KW):
-        barrier()
-        if k < KW - 1:
-            done(tt(T.acc[:], T.acc[:], tab(T.pr, k), add))
-            V.wait_ge(sem["t%d" % (k + 1)], 16)
-            done(tt(tab(T.pr, k + 1), tab(T.ts, k + 1), T.xp[:, k + 1:k + 1 + W], mult))
+    for i in range(KW):
+        V.wait_ge(sem["t%d" % i], 16)
+        ins = tt(col(T.pr, i), col(T.ts, SLOT[i]), T.xp[:, i:i + W], mult)
+        if i < KW - 1:
+            ins.then_inc(sem["p%d" % i], 1)
         else:
-            done(tt(T.ys[:], T.acc[:], tab(T.pr, k), add))
-
-    V.wait_ge(sem.hb, 32)
-    done(tt(T.pa[:, 0:2], T.ts[:, 0:2], T.hb[:, 0:2], mult))
-    done(tt(T.pa[:, 2:4], T.ts[:, KW * W - 2:KW * W], T.hb[:, 2:4], mult))
-    c1, c3 = W, 3 * W + W - 1
-    done(tt(T.pb[:, 0:2], T.ts[:, c1:c3 + 1:c3 - c1], T.hb[:, 1:3], mult))
+            done(ins)
+    V.wait_ge(sem.pe, 1)
     barrier()
-    done(tt(T.pa[:, 0:4:3], T.pa[:, 0:4:3], T.pb[:, 0:2], add))
-    barrier()
-    tt(T.ys[:, 0:2], T.ys[:, 0:2], T.pa[:, 0:2], add).then_inc(sem.vd, 1)
-    tt(T.ys[:, W - 2:W], T.ys[:, W - 2:W], T.pa[:, 2:4], add).then_inc(sem.vd, 1)
+    tt(T.ys[:], T.acc[:], col(T.pr, KW - 1), add).then_inc(sem.vi, 1)
 
+    V.wait_ge(sem.hb, 2 * NH)
+    done(tt(T.pa[:, 0:4], T.ts[:, W - 2:W + 2], T.hb[:, 0:4], mult))
+    done(tt(T.pb[:, 0:2], T.ts[:, 4 * W - 1:4 * W + 1], T.hb[:, 0:4:3], mult))
+    barrier()
+    done(tt(T.pa[:, 1:3], T.pa[:, 1:3], T.pb[:, 0:2], add))
+    barrier()
+    V.wait_ge(sem.vi, 1)
+    tt(T.ys[:, W - 2:W], T.ys[:, W - 2:W], T.pa[:, 0:2], add).then_inc(sem.vd, 1)
+    tt(T.ys[:, 0:2], T.ys[:, 0:2], T.pa[:, 2:4], add).then_inc(sem.vd, 1)
+
+    S.wait_ge(sem.vi, 1)
+    S.dma_start(T.y[:, H:W - H], T.ys[:, H:W - H]).then_inc(sem.st, 16)
     S.wait_ge(sem.vd, 2)
-    S.dma_start(T.y[:], T.ys[:]).then_inc(sem.st, 16)
-    S.wait_ge(sem.st, 16)
+    S.dma_start(T.y[:, 0:H], T.ys[:, 0:H]).then_inc(sem.st, 16)
+    A.wait_ge(sem.vd, 2)
+    A.dma_start(T.y[:, W - H:W], T.ys[:, W - H:W]).then_inc(sem.st, 16)
+    S.wait_ge(sem.st, 48)

@@ -1,15 +1,15 @@
 from concourse.bass import DstId, RemoteDMATransfer
-from concourse.mybir import AluOpType
+from concourse.mybir import AluOpType, ActivationFunctionType
 
 W, KW = 512, 5
 H = KW // 2
-NH = 4
+HW = W // 2
+NH = 8
 SLOT = {4: 0, 0: 1, 2: 2, 3: 3, 1: 4}
 
 SCRATCH = {
     "ed": ("dram", [2, 128, H], "bfloat16"),
     "rl": ("dram", [128, H], "bfloat16"),
-    "idd": ("dram", [1, 128 * 129], "bfloat16"),
     "hb": ("sbuf", [128, 8], "bfloat16"),
     "xs": ("sbuf", [128, W], "bfloat16"),
     "ts": ("sbuf", [128, KW * W], "bfloat16"),
@@ -17,13 +17,16 @@ SCRATCH = {
     "ys": ("sbuf", [128, W], "bfloat16"),
     "pa": ("sbuf", [128, 4], "float32"),
     "pb": ("sbuf", [128, 4], "float32"),
-    "zz": ("sbuf", [128, 136], "bfloat16"),
+    "on": ("sbuf", [128, 128], "bfloat16"),
     "idm": ("sbuf", [128, 128], "bfloat16"),
-    "xp": ("psum", [128, 2 * W], "float32"),
-    "acc": ("psum", [128, W], "float32"),
+    "xa": ("psum", [128, W], "float32"),
+    "xb": ("psum", [128, W], "float32"),
+    "acc0": ("psum", [128, W], "float32"),
+    "acc1": ("psum", [128, W], "float32"),
 }
-SEMAPHORES = ["ed", "x", "t0", "t1", "t2", "t3", "t4", "sent", "rl", "hb", "v", "vi", "vd", "st",
-              "ms", "i1", "idr", "p0", "p1", "p2", "p3", "pe"]
+SEMAPHORES = ["ed", "x", "t0", "t1", "t2", "t3", "t4a", "t4b", "sent", "rl", "hb", "v", "vi0", "vi1", "vd", "st",
+              "ms", "sel", "idr", "z", "xa", "xb", "gate", "pe0", "pe1",
+              "p0a", "p0b", "p1a", "p1b", "p2a", "p2b", "p3a", "p3b"]
 
 
 def _engines(mask, n, skip=0):
@@ -63,17 +66,31 @@ def rank_program(g, core, T, topo):
 
     for src, side, via, dst in routes:
         if via == core:
+            team = [r[2] for r in routes if r[0] == src and r[2] is not None]
+            wd = 128 // len(team)
+            c0 = wd * team.index(core)
+            eng = _engines(topo.mask(core, dst) & topo.mask(core, src), NH)
+            g.vector.memset(T.on[:, 0:wd], 1.0).then_inc(sem.ms, 1)
+            g.wait_ge(sem.ms, 1)
+            g.affine_select(out=T.idm[:, c0:c0 + wd], in_=T.on[:, 0:wd], pattern=[[-1, wd]],
+                            compare_op=AluOpType.is_equal, fill=0.0, base=-c0, channel_multiplier=1) \
+                .then_inc(sem.sel, 1)
+            g.wait_ge(sem.sel, 1)
+            rid, pid, _se = topo.addr(src)
+            g.remote_dma(out_ap=T.idm[:, c0:c0 + wd], in_ap=T.idm[:, c0:c0 + wd], remote_sem=sem.idr,
+                         local_sem=sem.sent, pid=pid, routing_id=rid, dma_engine_mask=eng)
             rid, pid, _se = topo.addr(dst)
             g.wait_ge(sem.rl, 1)
             g.remote_dma(out_ap=_landing(T, side), in_ap=T.rl[:], remote_sem=sem.hb, local_sem=sem.sent, pid=pid,
-                         routing_id=rid, dma_engine_mask=_engines(topo.mask(core, dst), NH))
-            g.wait_ge(sem.sent, NH)
+                         routing_id=rid, dma_engine_mask=eng)
+            g.wait_ge(sem.sent, 2 * NH)
             return
     if T.rank_of(core) is None:
         return
 
     S, A, V, P = g.sync, g.scalar, g.vector, g.tensor
     col = lambda b, j: b[:, W * j:W * j + W]
+    half = lambda b, j, h: b[:, W * j + HW * h:W * j + HW * h + HW]
 
     def load(q, i):
         q.dma_start(col(T.ts, SLOT[i]), col(T.t, i)).then_inc(sem["t%d" % i], 16)
@@ -81,15 +98,17 @@ def rank_program(g, core, T, topo):
     S.dma_start(T.ed[0], T.x[:, 0:H]).then_inc(sem.ed, 16)
     A.dma_start(T.ed[1], T.x[:, W - H:W]).then_inc(sem.ed, 16)
     S.dma_start(T.xs[:], T.x[:]).then_inc(sem.x, 16)
-    A.wait_ge(sem.ms, 2)
-    A.dma_start(T.idd[0], T.zz[:, 0:129]).then_inc(sem.i1, 16)
     load(A, 0)
-    load(A, 1)
-    load(A, 2)
-    A.wait_ge(sem.i1, 16)
-    A.dma_start(T.idm[:], T.idd[0, 0:128 * 128]).then_inc(sem.idr, 16)
-    load(A, 3)
-    load(A, 4)
+    load(S, 1)
+    S.wait_ge(sem.gate, 1)
+    load(S, 2)
+    load(S, 3)
+    A.wait_ge(sem.x, 16)
+    A.wait_ge(sem.z, 2)
+    A.activation(out=T.xb[:, 0:HW + H], in_=T.xs[:, HW - H:W], func=ActivationFunctionType.Copy).then_inc(sem.xb, 1)
+    A.wait_ge(sem.gate, 1)
+    A.dma_start(half(T.ts, SLOT[4], 0), half(T.t, 4, 0)).then_inc(sem.t4a, 16)
+    A.dma_start(half(T.ts, SLOT[4], 1), half(T.t, 4, 1)).then_inc(sem.t4b, 16)
 
     mine = [r for r in routes if r[0] == core]
     transfers = []
@@ -108,13 +127,18 @@ def rank_program(g, core, T, topo):
             g.remote_dma(out_ap=_landing(T, side), in_ap=T.ed[side], remote_sem=sem.hb, local_sem=sem.sent, pid=pid,
                          routing_id=rid, dma_engine_mask=_engines(topo.mask(core, dst), NH))
             left += NH
+    g.sem_inc(sem.gate, 1)
     g.wait_ge(sem.sent, left)
 
-    P.wait_ge(sem.idr, 16)
+    P.wait_ge(sem.idr, NH * len(transfers))
+    accs = (T.acc0, T.acc1)
     for j in range(KW - 1):
-        P.wait_ge(sem["p%d" % j], 1)
-        mm = P.matmul(out=T.acc[:], lhsT=T.idm[:], rhs=col(T.pr, j), start=(j == 0), stop=(j == KW - 2))
-    mm.then_inc(sem.pe, 1)
+        for h in (0, 1):
+            P.wait_ge(sem["p%d%s" % (j, "ab"[h])], 1)
+            mm = P.matmul(out=accs[h][:, 0:HW], lhsT=T.idm[:], rhs=half(T.pr, j, h), start=(j == 0),
+                          stop=(j == KW - 2))
+            if j == KW - 2:
+                mm.then_inc(sem["pe%d" % h], 1)
 
     issued = [0]
 
@@ -129,23 +153,26 @@ def rank_program(g, core, T, topo):
         return V.tensor_tensor(out=out, in0=in0, in1=in1, op=op)
 
     mult, add = AluOpType.mult, AluOpType.add
-    V.memset(T.zz[:, 1:129], 0.0).then_inc(sem.ms, 1)
-    V.memset(T.zz[:, 0:1], 1.0).then_inc(sem.ms, 1)
-    done(V.memset(T.xp[:, 0:H], 0.0))
-    done(V.memset(T.xp[:, W + H:W + 2 * H], 0.0))
+    xh = (T.xa, T.xb)
+    V.memset(T.xa[:, 0:H], 0.0).then_inc(sem.z, 1)
+    V.memset(T.xb[:, HW + H:HW + 2 * H], 0.0).then_inc(sem.z, 1)
     V.wait_ge(sem.x, 16)
-    done(V.tensor_copy(out=T.xp[:, H:W + H], in_=T.xs[:]))
-    barrier()
-    for i in range(KW):
+    V.wait_ge(sem.z, 2)
+    V.tensor_copy(out=T.xa[:, H:HW + 2 * H], in_=T.xs[:, 0:HW + H]).then_inc(sem.xa, 1)
+    for i in range(KW - 1):
         V.wait_ge(sem["t%d" % i], 16)
-        ins = tt(col(T.pr, i), col(T.ts, SLOT[i]), T.xp[:, i:i + W], mult)
-        if i < KW - 1:
-            ins.then_inc(sem["p%d" % i], 1)
-        else:
-            done(ins)
-    V.wait_ge(sem.pe, 1)
-    barrier()
-    tt(T.ys[:], T.acc[:], col(T.pr, KW - 1), add).then_inc(sem.vi, 1)
+        for h in (0, 1):
+            if i == 0:
+                V.wait_ge(sem["xa" if h == 0 else "xb"], 1)
+            tt(half(T.pr, i, h), half(T.ts, SLOT[i], h), xh[h][:, i:i + HW], mult) \
+                .then_inc(sem["p%d%s" % (i, "ab"[h])], 1)
+    i = KW - 1
+    for h in (0, 1):
+        V.wait_ge(sem["t4a" if h == 0 else "t4b"], 16)
+        done(tt(half(T.pr, i, h), half(T.ts, SLOT[i], h), xh[h][:, i:i + HW], mult))
+        V.wait_ge(sem["pe%d" % h], 1)
+        barrier()
+        tt(half(T.ys, 0, h), accs[h][:, 0:HW], half(T.pr, i, h), add).then_inc(sem["vi%d" % h], 1)
 
     V.wait_ge(sem.hb, 2 * NH)
     done(tt(T.pa[:, 0:4], T.ts[:, W - 2:W + 2], T.hb[:, 0:4], mult))
@@ -153,14 +180,17 @@ def rank_program(g, core, T, topo):
     barrier()
     done(tt(T.pa[:, 1:3], T.pa[:, 1:3], T.pb[:, 0:2], add))
     barrier()
-    V.wait_ge(sem.vi, 1)
+    V.wait_ge(sem.vi0, 1)
+    V.wait_ge(sem.vi1, 1)
     tt(T.ys[:, W - 2:W], T.ys[:, W - 2:W], T.pa[:, 0:2], add).then_inc(sem.vd, 1)
     tt(T.ys[:, 0:2], T.ys[:, 0:2], T.pa[:, 2:4], add).then_inc(sem.vd, 1)
 
-    S.wait_ge(sem.vi, 1)
-    S.dma_start(T.y[:, H:W - H], T.ys[:, H:W - H]).then_inc(sem.st, 16)
+    A.wait_ge(sem.vi0, 1)
+    A.dma_start(T.y[:, H:HW], T.ys[:, H:HW]).then_inc(sem.st, 16)
+    S.wait_ge(sem.vi1, 1)
+    S.dma_start(T.y[:, HW:W - H], T.ys[:, HW:W - H]).then_inc(sem.st, 16)
     S.wait_ge(sem.vd, 2)
     S.dma_start(T.y[:, 0:H], T.ys[:, 0:H]).then_inc(sem.st, 16)
     A.wait_ge(sem.vd, 2)
     A.dma_start(T.y[:, W - H:W], T.ys[:, W - H:W]).then_inc(sem.st, 16)
-    S.wait_ge(sem.st, 48)
+    S.wait_ge(sem.st, 64)

from concourse.bass import DstId, RemoteDMATransfer
from concourse.mybir import AluOpType, ActivationFunctionType

W, KW = 512, 5
H = KW // 2
HW = W // 2
NH = 8
SLOT = {4: 0, 0: 1, 2: 2, 3: 3, 1: 4}

SCRATCH = {
    "ed": ("dram", [2, 128, H], "bfloat16"),
    "rl": ("dram", [128, H], "bfloat16"),
    "hb": ("sbuf", [128, 8], "bfloat16"),
    "xs": ("sbuf", [128, W], "bfloat16"),
    "ts": ("sbuf", [128, KW * W], "bfloat16"),
    "pr": ("sbuf", [128, KW * W], "bfloat16"),
    "ys": ("sbuf", [128, W], "bfloat16"),
    "pa": ("sbuf", [128, 4], "float32"),
    "pb": ("sbuf", [128, 4], "float32"),
    "on": ("sbuf", [128, 128], "bfloat16"),
    "idm": ("sbuf", [128, 128], "bfloat16"),
    "xa": ("psum", [128, W], "float32"),
    "xb": ("psum", [128, W], "float32"),
    "acc0": ("psum", [128, W], "float32"),
    "acc1": ("psum", [128, W], "float32"),
}
SEMAPHORES = ["ed", "x", "t0", "t1", "t2", "t3", "t4a", "t4b", "sent", "rl", "hb", "v", "vi0", "vi1", "vd", "st",
              "ms", "sel", "idr", "z", "xa", "xb", "gate", "pe0", "pe1",
              "p0a", "p0b", "p1a", "p1b", "p2a", "p2b", "p3a", "p3b"]


def _engines(mask, n, skip=0):
    bits = [b for b in range(mask.bit_length()) if (mask >> b) & 1]
    m = 0
    for b in bits[skip:skip + n]:
        m |= 1 << b
    return m


def _routes(T, topo):
    cores = list(T.cores)
    n = len(cores)
    used = set(cores)
    out = []
    for r, src in enumerate(cores):
        for side in (0, 1):
            dst = cores[(r + (1 if side else -1)) % n]
            via = None
            if not topo.may_write(src, dst):
                cand = [h for h in range(topo.CHIPS * topo.CORES_PER_CHIP)
                        if topo.chip(h) == topo.chip(src) and h not in used and topo.may_write(h, dst)]
                cand.sort(key=lambda h: (topo.die(h) != topo.die(src), h))
                via = cand[0]
                used.add(via)
            out.append((src, side, via, dst))
    return out


def _landing(T, side):
    return T.hb[:, 0:H] if side == 0 else T.hb[:, H:2 * H]


def rank_program(g, core, T, topo):
    routes = _routes(T, topo)
    sem = T.sem

    for src, side, via, dst in routes:
        if via == core:
            team = [r[2] for r in routes if r[0] == src and r[2] is not None]
            wd = 128 // len(team)
            c0 = wd * team.index(core)
            eng = _engines(topo.mask(core, dst) & topo.mask(core, src), NH)
            g.vector.memset(T.on[:, 0:wd], 1.0).then_inc(sem.ms, 1)
            g.wait_ge(sem.ms, 1)
            g.affine_select(out=T.idm[:, c0:c0 + wd], in_=T.on[:, 0:wd], pattern=[[-1, wd]],
                            compare_op=AluOpType.is_equal, fill=0.0, base=-c0, channel_multiplier=1) \
                .then_inc(sem.sel, 1)
            g.wait_ge(sem.sel, 1)
            rid, pid, _se = topo.addr(src)
            g.remote_dma(out_ap=T.idm[:, c0:c0 + wd], in_ap=T.idm[:, c0:c0 + wd], remote_sem=sem.idr,
                         local_sem=sem.sent, pid=pid, routing_id=rid, dma_engine_mask=eng)
            rid, pid, _se = topo.addr(dst)
            g.wait_ge(sem.rl, 1)
            g.remote_dma(out_ap=_landing(T, side), in_ap=T.rl[:], remote_sem=sem.hb, local_sem=sem.sent, pid=pid,
                         routing_id=rid, dma_engine_mask=eng)
            g.wait_ge(sem.sent, 2 * NH)
            return
    if T.rank_of(core) is None:
        return

    S, A, V, P = g.sync, g.scalar, g.vector, g.tensor
    col = lambda b, j: b[:, W * j:W * j + W]
    half = lambda b, j, h: b[:, W * j + HW * h:W * j + HW * h + HW]

    def load(q, i):
        q.dma_start(col(T.ts, SLOT[i]), col(T.t, i)).then_inc(sem["t%d" % i], 16)

    S.dma_start(T.ed[0], T.x[:, 0:H]).then_inc(sem.ed, 16)
    A.dma_start(T.ed[1], T.x[:, W - H:W]).then_inc(sem.ed, 16)
    S.dma_start(T.xs[:], T.x[:]).then_inc(sem.x, 16)
    load(A, 0)
    load(S, 1)
    S.wait_ge(sem.gate, 1)
    load(S, 2)
    load(S, 3)
    A.wait_ge(sem.x, 16)
    A.wait_ge(sem.z, 2)
    A.activation(out=T.xb[:, 0:HW + H], in_=T.xs[:, HW - H:W], func=ActivationFunctionType.Copy).then_inc(sem.xb, 1)
    A.wait_ge(sem.gate, 1)
    A.dma_start(half(T.ts, SLOT[4], 0), half(T.t, 4, 0)).then_inc(sem.t4a, 16)
    A.dma_start(half(T.ts, SLOT[4], 1), half(T.t, 4, 1)).then_inc(sem.t4b, 16)

    mine = [r for r in routes if r[0] == core]
    transfers = []
    for src, side, via, dst in mine:
        if via is not None:
            rid, pid, _se = topo.addr(via)
            transfers.append(RemoteDMATransfer(dst_ids=[DstId(rid=rid, pnc=pid)],
                                               dma_engine_mask=_engines(topo.mask(core, via), 1, skip=side),
                                               remote_sem=sem.rl, src=T.ed[side], dst=T.rl[:]))
    g.wait_ge(sem.ed, 32)
    g.remote_dma_fused(transfers, local_sem=sem.sent)
    left = len(transfers)
    for src, side, via, dst in mine:
        if via is None:
            rid, pid, _se = topo.addr(dst)
            g.remote_dma(out_ap=_landing(T, side), in_ap=T.ed[side], remote_sem=sem.hb, local_sem=sem.sent, pid=pid,
                         routing_id=rid, dma_engine_mask=_engines(topo.mask(core, dst), NH))
            left += NH
    g.sem_inc(sem.gate, 1)
    g.wait_ge(sem.sent, left)

    P.wait_ge(sem.idr, NH * len(transfers))
    accs = (T.acc0, T.acc1)
    for j in range(KW - 1):
        for h in (0, 1):
            P.wait_ge(sem["p%d%s" % (j, "ab"[h])], 1)
            mm = P.matmul(out=accs[h][:, 0:HW], lhsT=T.idm[:], rhs=half(T.pr, j, h), start=(j == 0),
                          stop=(j == KW - 2))
            if j == KW - 2:
                mm.then_inc(sem["pe%d" % h], 1)

    issued = [0]

    def done(ins):
        ins.then_inc(sem.v, 1)
        issued[0] += 1

    def barrier():
        V.wait_ge(sem.v, issued[0])

    def tt(out, in0, in1, op):
        return V.tensor_tensor(out=out, in0=in0, in1=in1, op=op)

    mult, add = AluOpType.mult, AluOpType.add
    xh = (T.xa, T.xb)
    V.memset(T.xa[:, 0:H], 0.0).then_inc(sem.z, 1)
    V.memset(T.xb[:, HW + H:HW + 2 * H], 0.0).then_inc(sem.z, 1)
    V.wait_ge(sem.x, 16)
    V.wait_ge(sem.z, 2)
    V.tensor_copy(out=T.xa[:, H:HW + 2 * H], in_=T.xs[:, 0:HW + H]).then_inc(sem.xa, 1)
    for i in range(KW - 1):
        V.wait_ge(sem["t%d" % i], 16)
        for h in (0, 1):
            if i == 0:
                V.wait_ge(sem["xa" if h == 0 else "xb"], 1)
            tt(half(T.pr, i, h), half(T.ts, SLOT[i], h), xh[h][:, i:i + HW], mult) \
                .then_inc(sem["p%d%s" % (i, "ab"[h])], 1)
    i = KW - 1
    for h in (0, 1):
        V.wait_ge(sem["t4a" if h == 0 else "t4b"], 16)
        done(tt(half(T.pr, i, h), half(T.ts, SLOT[i], h), xh[h][:, i:i + HW], mult))
        V.wait_ge(sem["pe%d" % h], 1)
        barrier()
        tt(half(T.ys, 0, h), accs[h][:, 0:HW], half(T.pr, i, h), add).then_inc(sem["vi%d" % h], 1)

    V.wait_ge(sem.hb, 2 * NH)
    done(tt(T.pa[:, 0:4], T.ts[:, W - 2:W + 2], T.hb[:, 0:4], mult))
    done(tt(T.pb[:, 0:2], T.ts[:, 4 * W - 1:4 * W + 1], T.hb[:, 0:4:3], mult))
    barrier()
    done(tt(T.pa[:, 1:3], T.pa[:, 1:3], T.pb[:, 0:2], add))
    barrier()
    V.wait_ge(sem.vi0, 1)
    V.wait_ge(sem.vi1, 1)
    tt(T.ys[:, W - 2:W], T.ys[:, W - 2:W], T.pa[:, 0:2], add).then_inc(sem.vd, 1)
    tt(T.ys[:, 0:2], T.ys[:, 0:2], T.pa[:, 2:4], add).then_inc(sem.vd, 1)

    A.wait_ge(sem.vi0, 1)
    A.dma_start(T.y[:, H:HW], T.ys[:, H:HW]).then_inc(sem.st, 16)
    S.wait_ge(sem.vi1, 1)
    S.dma_start(T.y[:, HW:W - H], T.ys[:, HW:W - H]).then_inc(sem.st, 16)
    S.wait_ge(sem.vd, 2)
    S.dma_start(T.y[:, 0:H], T.ys[:, 0:H]).then_inc(sem.st, 16)
    A.wait_ge(sem.vd, 2)
    A.dma_start(T.y[:, W - H:W], T.ys[:, W - H:W]).then_inc(sem.st, 16)
    S.wait_ge(sem.st, 64)
